import numpy as np
import ml_dtypes


def mxq(x, axis, fmt="e4m3"):
    dtype, down = {"e4m3": (ml_dtypes.float8_e4m3fn, 7), "e5m2": (ml_dtypes.float8_e5m2, 14)}[fmt]
    v = np.moveaxis(np.asarray(x, np.float32).astype(ml_dtypes.bfloat16).astype(np.float64), axis, -1)
    blocks = v.reshape(v.shape[:-1] + (-1, 32))
    amax = np.abs(blocks).max(-1, keepdims=True)
    byte = np.maximum(np.where(amax > 0, np.frexp(amax)[1] - 1 + 127, 0) - down, 1)
    scale = np.exp2(byte - 127.0)
    codes = (blocks / scale).astype(np.float32).astype(dtype).astype(np.float64)
    return np.moveaxis((codes * scale).reshape(v.shape), -1, axis)


WIDE = False


def mx_kscale(k):
    if not WIDE:
        return np.ones(k)
    levels = np.array([10, -10, 5, -5, 0])
    if k % 512:
        return np.exp2(np.random.permutation(np.resize(levels, k // 32))).repeat(32)
    a = np.empty((k // 512, 16))
    for p in range(k // 512):
        a[p, :8] = np.random.permutation(np.resize(levels, 8))
        for g in range(8):
            far = levels[np.abs(levels - a[p, g]) >= 10]
            a[p, g + 8] = far[np.random.randint(len(far))]
    return np.exp2(a.ravel()).repeat(32)


BF16 = ml_dtypes.bfloat16


def bf(x):
    return np.asarray(x, np.float32).astype(BF16)


def f64(x):
    return np.asarray(x).astype(np.float64)


B, N, D, M = 4, 1024, 256, 512
M2 = 2 * M


def draw0():
    s, t = mx_kscale(N), mx_kscale(M2)
    return {"v": bf(np.random.standard_normal((B, N, D)) * s[None, :, None]),
            "enc": bf(np.random.standard_normal((M2, N)) / np.sqrt(N) / s[None, :]),
            "dec": bf(np.random.standard_normal((N, M2)) / np.sqrt(M2) / t[None, :]),
            "alpha": bf(0.5 + 0.5 * np.random.standard_normal((M, D))),
            "omega": bf(np.random.standard_normal(M)),
            "beta": bf(np.random.standard_normal((M2, D)) * t[:, None])}


def pole_response(alpha, omega):
    s = np.log1p(np.exp(alpha))
    w = omega[:, None]
    den = s * s + w * w
    return s / den, -w / den


def core(v, enc, dec, alpha, omega, beta):
    m = omega.shape[0]
    c = mxq(f64(enc), 1, "e4m3") @ mxq(f64(v), 1, "e4m3")
    cr = c[:, :m, :]
    ci = c[:, m:, :]
    hr, hi = pole_response(f64(alpha), f64(omega))
    yr = cr * hr - ci * hi
    yi = cr * hi + ci * hr
    z = np.concatenate([yr, yi], axis=1) * f64(beta)
    return mxq(f64(dec), 1, "e4m3") @ mxq(z, 1, "e4m3")


def e4m3fn_bytes(y):
    return np.clip(np.asarray(y, np.float64), -448.0, 448.0).astype(np.float32).astype(ml_dtypes.float8_e4m3fn).view(np.uint8)


def e4m3fn_values(b):
    return np.asarray(b, np.uint8).view(ml_dtypes.float8_e4m3fn).astype(np.float64)


def setup_inputs():
    d = draw0()
    x0 = np.asarray(d['v']).astype(np.float64)
    s = (np.max(np.abs(x0), axis=(0, 2), keepdims=True) / 448.0).astype(np.float32)
    out = {}
    for k, v in d.items():
        if k == 'v':
            out['v_bytes'] = e4m3fn_bytes(x0 / s.astype(np.float64))
            out['v_scale'] = s
        else:
            out[k] = v
    return out


def reference(v_bytes, v_scale, enc, dec, alpha, omega, beta):
    return core(e4m3fn_values(v_bytes) * v_scale.astype(np.float64), enc, dec, alpha, omega, beta)

@@ -1,0 +1,448 @@
+from contextlib import ExitStack
+
+import concourse.mybir as mybir
+from concourse.masks import make_identity
+
+B, N, D, M = 4, 1024, 256, 512
+M2 = 2 * M
+P = 128
+PACK = 4
+HALF = 128
+
+FLOPS = 2 * B * D * (M2 * N + N * M2)
+
+F32 = mybir.dt.float32
+BF16 = mybir.dt.bfloat16
+U32 = mybir.dt.uint32
+U8 = mybir.dt.uint8
+FP8 = mybir.dt.float8_e4m3fn
+FP8X4 = mybir.dt.float8_e4m3fn_x4
+ACT = mybir.ActivationFunctionType
+ALU = mybir.AluOpType
+
+ALPHA_CAP = 40.0
+
+
+def tile_laplacepoleresidueoperator_kernel(tc, v_bytes, v_scale, enc, dec, alpha, omega, beta, out):
+    nc = tc.nc
+    enc_rows = enc.rearrange("(h p t) k -> h p t k", h=2, t=PACK)
+    dec_rows = dec.rearrange("(p j) k -> p j k", j=8)
+    out_rows = out.rearrange("b (p j) d -> b p j d", j=8)
+
+    with ExitStack() as ctx:
+        keep = ctx.enter_context(tc.tile_pool(name="keep", bufs=1))
+        work = ctx.enter_context(tc.tile_pool(name="work", bufs=2))
+        psum = ctx.enter_context(tc.psum_pool(name="psum", bufs=8))
+        ctx.enter_context(tc.manual_schedule())
+
+        v_sc = keep.tile([P, 2, PACK], F32, name="v_sc")
+        om = keep.tile([P, PACK], BF16, name="om")
+        warm = keep.tile([P, 2], F32, name="warm")
+        ident = keep.tile([P, P], F32, name="ident")
+        ident_b = keep.tile([P, P], BF16, name="ident_b")
+        al = keep.tile([P, PACK, D], BF16, name="al")
+        be = keep.tile([P, 2, PACK, D], BF16, name="be")
+        v_raw = []
+        for b in range(B):
+            v_raw.append(keep.tile([P, 2, PACK, D], U8, name="v_raw%d" % b))
+        raw = {}
+        for i in range(8):
+            raw["enc", i] = keep.tile([P, N], BF16, name="enc_raw%d" % i)
+            raw["dec", i] = keep.tile([P, M2], BF16, name="dec_raw%d" % i)
+        E = keep.tile([P, PACK, D], F32, name="E")
+        sp = keep.tile([P, PACK, D], F32, name="sp")
+        W = keep.tile([P, PACK, D], F32, name="W")
+        G = keep.tile([P, D, PACK], F32, name="G")
+        Gb = []
+        for g in range(2):
+            Gb.append(keep.tile([P, D, PACK], F32, name="Gb%d" % g))
+        capped = keep.tile([P, PACK, D], BF16, name="capped")
+        omf = keep.tile([P, PACK], F32, name="omf")
+        nom = keep.tile([P, PACK], F32, name="nom")
+        om2 = keep.tile([P, PACK], F32, name="om2")
+
+        banks, pairs, codes, scales, wide, mixed, us, z, results = {}, {}, {}, {}, {}, {}, {}, {}, {}
+        for kind in ("enc", "dec", "v", "z"):
+            for i in range(4):
+                codes[kind, i] = keep.tile([P, 2 * D], U32, name="c_%s_%d" % (kind, i), align_bytes=64)
+                scales[kind, i] = keep.tile([P, 2 * D], U8, name="s_%s_%d" % (kind, i), align_bytes=64)
+
+        def setup():
+            nc.scalar.dma_start(out=v_sc[:], in_=v_scale.rearrange("o (g p t) x -> p (o g) (t x)", p=P, t=PACK))
+            nc.scalar.dma_start(out=om[:], in_=omega.rearrange("(p t) -> p t", t=PACK))
+            nc.vector.memset(warm[:], 0.0)
+            nc.scalar.activation(out=warm[:, 1:2], in_=warm[:, 0:1], func=ACT.Exp)
+            make_identity(nc, ident[:])
+            make_identity(nc, ident_b[:])
+            nc.gpsimd.tensor_scalar(out=omf[:], in0=om[:], scalar1=1.0, scalar2=0.0, op0=ALU.mult, op1=ALU.add)
+            nc.gpsimd.tensor_scalar(out=nom[:], in0=om[:], scalar1=-1.0, scalar2=0.0, op0=ALU.mult, op1=ALU.add)
+            nc.gpsimd.tensor_tensor(out=om2[:], in0=om[:], in1=om[:], op=ALU.mult)
+
+        def load_alpha():
+            nc.sync.dma_start(out=al[:], in_=alpha.rearrange("(p t) d -> p t d", t=PACK))
+
+        def load_beta():
+            nc.sync.dma_start(out=be[:], in_=beta.rearrange("(g p t) d -> p g t d", p=P, t=PACK))
+
+        def load_v(b):
+            nc.sync.dma_start(
+                out=v_raw[b][:].rearrange("p g t d -> p g (t d)"),
+                in_=v_bytes[b].rearrange("(g p t) d -> p g (t d)", p=P, t=PACK),
+            )
+
+        def load_rows(kind, i):
+            src = enc_rows[i // 4][:, i % 4, :] if kind == "enc" else dec_rows[:, i, :]
+            nc.sync.dma_start(out=raw[kind, i][:], in_=src)
+
+        def flip(kind, i):
+            bank = psum.tile([P, 2, 2, P], F32, name="bank")
+            words = raw[kind, i][:].bitcast(F32)
+            for g in range(2):
+                for u in range(2):
+                    nc.tensor.transpose(bank[:, g, u, :], words[:, 256 * g + u : 256 * (g + 1) : 2], ident[:])
+            banks[kind, i] = bank
+
+        def unflip(kind, i, engine):
+            if (kind, i // 2) not in pairs:
+                pairs[kind, i // 2] = work.tile([P, 2, 2, P, PACK], BF16, name="pair", bufs=4, align_bytes=64)
+            dst = pairs[kind, i // 2][:, i % 2].bitcast(F32)
+            src = banks[kind, i][:].rearrange("p g u m -> p g m u")
+            if engine == "v":
+                nc.vector.tensor_copy(out=dst, in_=src)
+            else:
+                nc.scalar.copy(out=dst, in_=src)
+
+        def quantize(key, src, cols=slice(0, 2 * D)):
+            nc.vector.quantize_mx(out=codes[key][:, cols].bitcast(FP8X4), scales=scales[key][:, cols], in_=src)
+
+        def quantize_pair(kind, i):
+            quantize((kind, i), pairs[kind, i][:].rearrange("p e g m t -> p (e g m t)"))
+
+        def widen(b, g, engine):
+            if b not in wide:
+                wide[b] = work.tile([P, 2, PACK, D], BF16, name="wide")
+            for t in range(PACK):
+                src = v_raw[b][:, g, t, :].bitcast(FP8)
+                if engine == "v":
+                    nc.vector.tensor_scalar(out=wide[b][:, g, t, :], in0=src, scalar1=v_sc[:, g, t : t + 1], scalar2=None, op0=ALU.mult)
+                else:
+                    nc.scalar.activation(out=wide[b][:, g, t, :], in_=src, func=ACT.Copy, scale=v_sc[:, g, t : t + 1])
+
+        def mix(b, g):
+            bank = psum.tile([P, PACK, D], BF16, name="bank")
+            for q in range(2):
+                nc.tensor.matmul(
+                    bank[:, 2 * q : 2 * q + 2, :].rearrange("p t d -> p (t d)"),
+                    lhsT=ident_b[:],
+                    rhs=wide[b][:, g, 2 * q : 2 * q + 2, :].rearrange("p t d -> p (t d)"),
+                    start=True,
+                    stop=True,
+                )
+            banks["mix", b, g] = bank
+
+        def unmix(b, g):
+            if b not in mixed:
+                mixed[b] = work.tile([P, 2, D, PACK], BF16, name="mixed", align_bytes=64)
+            nc.scalar.copy(out=mixed[b][:, g], in_=banks["mix", b, g][:].rearrange("p t d -> p d t"))
+
+        def quantize_v(b):
+            quantize(("v", b), mixed[b][:].rearrange("p g d t -> p (g d t)"))
+
+        def shape(k):
+            b = k // 2
+            if b < 3:
+                return b, slice(2 * (k % 2), 2 * (k % 2) + 2), slice(0, D)
+            return b, slice(0, PACK), slice((k % 2) * HALF, (k % 2 + 1) * HALF)
+
+        def product(bank, i, kind, row, src, cols0, width):
+            for g in range(2):
+                w = slice((row % 2) * 256 + g * P, (row % 2) * 256 + (g + 1) * P)
+                c = slice(g * D + cols0, g * D + cols0 + width)
+                nc.tensor.matmul_mx(
+                    out=bank[:, i, :],
+                    lhsT=codes[kind, row // 2][:, w].bitcast(FP8X4),
+                    lhsT_scale=scales[kind, row // 2][:, w],
+                    rhs=codes[src][:, c].bitcast(FP8X4),
+                    rhs_scale=scales[src][:, c],
+                    start=(g == 0),
+                    stop=(g == 1),
+                )
+
+        def stage1(k, h):
+            b, ts, ds = shape(k)
+            nt, nd = ts.stop - ts.start, ds.stop - ds.start
+            bank = psum.tile([P, nt, nd], F32, name="bank")
+            for i in range(nt):
+                product(bank, i, "enc", 4 * h + ts.start + i, ("v", b), ds.start, nd)
+            banks["c", k, h] = bank
+
+        def cap():
+            nc.vector.tensor_scalar(out=capped[:], in0=al[:], scalar1=ALPHA_CAP, scalar2=None, op0=ALU.min)
+
+        def expo():
+            nc.scalar.activation(out=E[:], in_=capped[:], func=ACT.Exp)
+
+        def loga():
+            nc.scalar.activation(out=E[:], in_=E[:], func=ACT.Ln, bias=1.0)
+
+        def softplus():
+            nc.vector.tensor_tensor(out=sp[:], in0=E[:], in1=al[:], op=ALU.max)
+
+        def square():
+            nc.scalar.activation(out=W[:], in_=sp[:], func=ACT.Square)
+
+        def log_den():
+            for t in range(PACK):
+                nc.scalar.activation(out=W[:, t], in_=W[:, t], func=ACT.Ln, bias=om2[:, t : t + 1])
+
+        def inv_den():
+            nc.scalar.activation(out=G[:], in_=W[:].rearrange("p t d -> p d t"), func=ACT.Exp, scale=-1.0)
+
+        def gain(g, engine):
+            eng = nc.gpsimd if engine == "g" else nc.vector
+            eng.tensor_tensor(out=Gb[g][:], in0=G[:], in1=be[:, g].rearrange("p t d -> p d t"), op=ALU.mult)
+
+        def rotate_a(k, h):
+            b, ts, ds = shape(k)
+            if b not in us:
+                us[b] = work.tile([P, 2, PACK, D], F32, name="u")
+            nc.vector.tensor_tensor(out=us[b][:, h, ts, ds], in0=banks["c", k, h][:], in1=sp[:, ts, ds], op=ALU.mult)
+
+        def rotate_b(k, h):
+            b, ts, ds = shape(k)
+            other = banks["c", k, 1 - h]
+            for t in range(ts.start, ts.stop):
+                nc.vector.scalar_tensor_tensor(
+                    out=us[b][:, h, t, ds],
+                    in0=other[:, t - ts.start, :],
+                    scalar=(omf, nom)[h][:, t : t + 1],
+                    in1=us[b][:, h, t, ds],
+                    op0=ALU.mult,
+                    op1=ALU.add,
+                )
+
+        def unit(k):
+            for h in range(2):
+                rotate_a(k, h)
+            for h in range(2):
+                rotate_b(k, h)
+
+        def respond(b, n0, nd, g, engine):
+            if (b, n0) not in z:
+                z[b, n0] = work.tile([P, 2, nd * PACK], BF16, name="z%d" % nd, align_bytes=64)
+            eng = nc.gpsimd if engine == "g" else nc.vector
+            eng.tensor_tensor(
+                out=z[b, n0][:, g].rearrange("p (n t) -> p n t", t=PACK),
+                in0=us[b][:, g, :, n0 : n0 + nd].rearrange("p t n -> p n t"),
+                in1=Gb[g][:, n0 : n0 + nd, :],
+                op=ALU.mult,
+            )
+
+        def quantize_z(b, n0, nd):
+            if nd == D:
+                quantize(("z", b), z[b, n0][:].rearrange("p g n -> p (g n)"))
+            else:
+                for g in range(2):
+                    quantize(("z", b), z[b, n0][:, g, :], slice(g * D + n0, g * D + n0 + nd))
+
+        def stage2(b, n0, width, q):
+            per = 512 // width
+            bank = psum.tile([P, per, width], F32, name="bank")
+            for i in range(per):
+                product(bank, i, "dec", q * per + i, ("z", b), n0, width)
+            banks["o", b, n0, q] = bank
+
+        def finish(b, n0, width, q, engine):
+            if (b, n0) not in results:
+                results[b, n0] = work.tile([P, 8, width], F32, name="res%d" % width, bufs=2)
+            per = 512 // width
+            dst, src = results[b, n0][:, q * per : (q + 1) * per, :], banks["o", b, n0, q][:]
+            if engine == "v":
+                nc.vector.tensor_copy(out=dst, in_=src)
+            else:
+                nc.scalar.copy(out=dst, in_=src)
+
+        def store(b, n0, width, s):
+            nc.sync.dma_start(out=out_rows[b][:, 4 * s : 4 * s + 4, n0 : n0 + width], in_=results[b, n0][:, 4 * s : 4 * s + 4, :])
+
+        setup()
+        load_alpha()
+        load_v(1)
+        load_rows("enc", 6)
+        cap()
+        flip("enc", 6)
+        load_v(0)
+        widen(1, 1, "v")
+        load_rows("enc", 0)
+        mix(1, 1)
+        widen(1, 0, "v")
+        widen(0, 1, "v")
+        expo()
+        flip("enc", 0)
+        loga()
+        load_rows("enc", 3)
+        load_rows("enc", 2)
+        load_v(2)
+        flip("enc", 3)
+        widen(0, 0, "v")
+        unflip("enc", 6, "v")
+        mix(1, 0)
+        unflip("enc", 0, "v")
+        load_rows("enc", 1)
+        unmix(1, 1)
+        load_rows("enc", 4)
+        flip("enc", 2)
+        load_rows("enc", 7)
+        flip("enc", 1)
+        load_rows("enc", 5)
+        load_beta()
+        load_v(3)
+        unmix(1, 0)
+        unflip("enc", 3, "v")
+        unflip("enc", 2, "s")
+        softplus()
+        square()
+        flip("enc", 7)
+        quantize_v(1)
+        unflip("enc", 1, "v")
+        load_rows("dec", 5)
+        quantize_pair("enc", 1)
+        unflip("enc", 7, "v")
+        mix(0, 1)
+        flip("enc", 5)
+        unmix(0, 1)
+        flip("enc", 4)
+        unflip("enc", 5, "v")
+        mix(0, 0)
+        flip("dec", 5)
+        log_den()
+        unflip("enc", 4, "v")
+        unmix(0, 0)
+        quantize_pair("enc", 0)
+        quantize_pair("enc", 3)
+        load_rows("dec", 6)
+        stage1(3, 0)
+        inv_den()
+        gain(0, "g")
+        quantize_pair("enc", 2)
+        stage1(3, 1)
+        quantize_v(0)
+        widen(3, 1, "s")
+        load_rows("dec", 3)
+        flip("dec", 3)
+        unflip("dec", 5, "s")
+        load_rows("dec", 4)
+        stage1(2, 1)
+        widen(3, 0, "s")
+        stage1(2, 0)
+        unit(3)
+        stage1(1, 1)
+        mix(3, 1)
+        unflip("dec", 3, "s")
+        stage1(1, 0)
+        load_rows("dec", 7)
+        gain(1, "g")
+        unit(2)
+        unit(1)
+        widen(2, 1, "s")
+        stage1(0, 1)
+        stage1(0, 0)
+        flip("dec", 6)
+        respond(1, 0, 256, 0, "g")
+        load_rows("dec", 1)
+        unflip("dec", 6, "s")
+        unit(0)
+        widen(2, 0, "s")
+        mix(3, 0)
+        unmix(3, 1)
+        load_rows("dec", 2)
+        unmix(3, 0)
+        quantize_v(3)
+        flip("dec", 7)
+        load_rows("dec", 0)
+        unflip("dec", 7, "s")
+        mix(2, 1)
+        unmix(2, 1)
+        respond(1, 0, 256, 1, "g")
+        flip("dec", 4)
+        mix(2, 0)
+        flip("dec", 1)
+        stage1(7, 0)
+        stage1(7, 1)
+        respond(0, 0, 256, 1, "g")
+        unmix(2, 0)
+        stage1(6, 1)
+        quantize_pair("dec", 3)
+        stage1(6, 0)
+        quantize_v(2)
+        unflip("dec", 4, "s")
+        flip("dec", 2)
+        quantize_z(1, 0, 256)
+        unit(7)
+        flip("dec", 0)
+        unit(6)
+        unflip("dec", 1, "s")
+        quantize_pair("dec", 2)
+        unflip("dec", 2, "s")
+        stage1(4, 1)
+        respond(0, 0, 256, 0, "g")
+        quantize_z(0, 0, 256)
+        stage1(4, 0)
+        unflip("dec", 0, "s")
+        unit(4)
+        respond(3, 0, 128, 1, "g")
+        stage2(0, 0, 256, 2)
+        stage2(1, 0, 256, 2)
+        stage2(0, 0, 256, 3)
+        stage1(5, 1)
+        respond(3, 0, 128, 0, "g")
+        quantize_pair("dec", 1)
+        finish(0, 0, 256, 3, "s")
+        quantize_pair("dec", 0)
+        finish(0, 0, 256, 2, "s")
+        stage1(5, 0)
+        stage2(0, 0, 256, 1)
+        stage2(0, 0, 256, 0)
+        finish(1, 0, 256, 2, "s")
+        store(0, 0, 256, 1)
+        stage2(1, 0, 256, 3)
+        finish(0, 0, 256, 0, "s")
+        stage2(1, 0, 256, 1)
+        finish(1, 0, 256, 3, "s")
+        finish(1, 0, 256, 1, "s")
+        finish(0, 0, 256, 1, "s")
+        respond(3, 128, 128, 0, "g")
+        unit(5)
+        quantize_z(3, 0, 128)
+        stage2(1, 0, 256, 0)
+        finish(1, 0, 256, 0, "s")
+        stage2(3, 0, 128, 0)
+        finish(3, 0, 128, 0, "s")
+        store(1, 0, 256, 1)
+        respond(3, 128, 128, 1, "g")
+        stage2(3, 0, 128, 1)
+        store(0, 0, 256, 0)
+        store(3, 0, 128, 0)
+        quantize_z(3, 128, 128)
+        respond(2, 0, 256, 0, "v")
+        store(1, 0, 256, 0)
+        stage2(3, 128, 128, 0)
+        finish(3, 0, 128, 1, "s")
+        finish(3, 128, 128, 0, "s")
+        respond(2, 0, 256, 1, "v")
+        stage2(3, 128, 128, 1)
+        store(3, 0, 128, 1)
+        quantize_z(2, 0, 256)
+        stage2(2, 0, 256, 3)
+        finish(3, 128, 128, 1, "s")
+        finish(2, 0, 256, 3, "s")
+        store(3, 128, 128, 1)
+        stage2(2, 0, 256, 2)
+        stage2(2, 0, 256, 0)
+        store(3, 128, 128, 0)
+        finish(2, 0, 256, 2, "s")
+        store(2, 0, 256, 1)
+        finish(2, 0, 256, 0, "s")
+        stage2(2, 0, 256, 1)
+        finish(2, 0, 256, 1, "s")
+        store(2, 0, 256, 0)

@@ -46,9 +46,9 @@ def tile_laplacepoleresidueoperator_kernel(tc, v_bytes, v_scale, enc, dec, alpha
         for b in range(B):
             v_raw.append(keep.tile([P, 2, PACK, D], U8, name="v_raw%d" % b))
         raw = {}
-        for i in range(8):
-            raw["enc", i] = keep.tile([P, N], BF16, name="enc_raw%d" % i)
-            raw["dec", i] = keep.tile([P, M2], BF16, name="dec_raw%d" % i)
+        for i in range(4):
+            raw["enc", i] = keep.tile([P, 2, N], BF16, name="enc_raw%d" % i)
+            raw["dec", i] = keep.tile([P, 2, M2], BF16, name="dec_raw%d" % i)
         E = keep.tile([P, PACK, D], F32, name="E")
         sp = keep.tile([P, PACK, D], F32, name="sp")
         W = keep.tile([P, PACK, D], F32, name="W")
@@ -91,12 +91,13 @@ def tile_laplacepoleresidueoperator_kernel(tc, v_bytes, v_scale, enc, dec, alpha
             )
 
         def load_rows(kind, i):
-            src = enc_rows[i // 4][:, i % 4, :] if kind == "enc" else dec_rows[:, i, :]
+            j = 2 * (i % 2) if kind == "enc" else 2 * i
+            src = (enc_rows[i // 2] if kind == "enc" else dec_rows)[:, j : j + 2, :]
             nc.sync.dma_start(out=raw[kind, i][:], in_=src)
 
         def flip(kind, i):
             bank = psum.tile([P, 2, 2, P], F32, name="bank")
-            words = raw[kind, i][:].bitcast(F32)
+            words = raw[kind, i // 2][:, i % 2].bitcast(F32)
             for g in range(2):
                 for u in range(2):
                     nc.tensor.transpose(bank[:, g, u, :], words[:, 256 * g + u : 256 * (g + 1) : 2], ident[:])
@@ -267,182 +268,174 @@ def tile_laplacepoleresidueoperator_kernel(tc, v_bytes, v_scale, enc, dec, alpha
 
         setup()
         load_alpha()
-        load_v(1)
-        load_rows("enc", 6)
         cap()
-        flip("enc", 6)
-        load_v(0)
-        widen(1, 1, "v")
-        load_rows("enc", 0)
-        mix(1, 1)
-        widen(1, 0, "v")
-        widen(0, 1, "v")
         expo()
-        flip("enc", 0)
-        loga()
-        load_rows("enc", 3)
-        load_rows("enc", 2)
-        load_v(2)
-        flip("enc", 3)
+        load_v(0)
+        load_rows("enc", 0)
         widen(0, 0, "v")
-        unflip("enc", 6, "v")
-        mix(1, 0)
-        unflip("enc", 0, "v")
-        load_rows("enc", 1)
-        unmix(1, 1)
-        load_rows("enc", 4)
-        flip("enc", 2)
-        load_rows("enc", 7)
+        flip("enc", 0)
         flip("enc", 1)
-        load_rows("enc", 5)
-        load_beta()
-        load_v(3)
-        unmix(1, 0)
-        unflip("enc", 3, "v")
-        unflip("enc", 2, "s")
-        softplus()
-        square()
-        flip("enc", 7)
-        quantize_v(1)
-        unflip("enc", 1, "v")
-        load_rows("dec", 5)
-        quantize_pair("enc", 1)
-        unflip("enc", 7, "v")
-        mix(0, 1)
-        flip("enc", 5)
-        unmix(0, 1)
-        flip("enc", 4)
-        unflip("enc", 5, "v")
+        loga()
         mix(0, 0)
-        flip("dec", 5)
-        log_den()
-        unflip("enc", 4, "v")
+        widen(0, 1, "v")
+        mix(0, 1)
+        load_rows("enc", 2)
         unmix(0, 0)
+        flip("enc", 4)
+        unmix(0, 1)
+        load_rows("enc", 1)
+        flip("enc", 5)
+        unflip("enc", 0, "v")
+        unflip("enc", 1, "v")
+        unflip("enc", 4, "s")
+        load_rows("enc", 3)
+        load_v(1)
         quantize_pair("enc", 0)
-        quantize_pair("enc", 3)
-        load_rows("dec", 6)
-        stage1(3, 0)
-        inv_den()
-        gain(0, "g")
-        quantize_pair("enc", 2)
-        stage1(3, 1)
+        flip("enc", 2)
+        flip("enc", 3)
+        flip("enc", 6)
+        unflip("enc", 5, "s")
+        softplus()
         quantize_v(0)
-        widen(3, 1, "s")
-        load_rows("dec", 3)
-        flip("dec", 3)
-        unflip("dec", 5, "s")
-        load_rows("dec", 4)
-        stage1(2, 1)
-        widen(3, 0, "s")
-        stage1(2, 0)
-        unit(3)
-        stage1(1, 1)
-        mix(3, 1)
-        unflip("dec", 3, "s")
-        stage1(1, 0)
-        load_rows("dec", 7)
-        gain(1, "g")
-        unit(2)
-        unit(1)
-        widen(2, 1, "s")
-        stage1(0, 1)
+        load_beta()
+        unflip("enc", 3, "s")
+        widen(1, 0, "v")
+        square()
+        quantize_pair("enc", 2)
+        load_v(2)
+        load_v(3)
+        flip("enc", 7)
+        widen(1, 1, "v")
         stage1(0, 0)
-        flip("dec", 6)
-        respond(1, 0, 256, 0, "g")
-        load_rows("dec", 1)
-        unflip("dec", 6, "s")
+        stage1(0, 1)
         unit(0)
-        widen(2, 0, "s")
-        mix(3, 0)
-        unmix(3, 1)
-        load_rows("dec", 2)
-        unmix(3, 0)
-        quantize_v(3)
-        flip("dec", 7)
+        unflip("enc", 7, "s")
         load_rows("dec", 0)
-        unflip("dec", 7, "s")
-        mix(2, 1)
-        unmix(2, 1)
-        respond(1, 0, 256, 1, "g")
-        flip("dec", 4)
-        mix(2, 0)
-        flip("dec", 1)
-        stage1(7, 0)
-        stage1(7, 1)
-        respond(0, 0, 256, 1, "g")
-        unmix(2, 0)
-        stage1(6, 1)
-        quantize_pair("dec", 3)
-        stage1(6, 0)
-        quantize_v(2)
-        unflip("dec", 4, "s")
-        flip("dec", 2)
-        quantize_z(1, 0, 256)
-        unit(7)
+        unflip("enc", 2, "s")
+        mix(1, 0)
+        unmix(1, 0)
+        quantize_pair("enc", 1)
+        mix(1, 1)
         flip("dec", 0)
-        unit(6)
-        unflip("dec", 1, "s")
-        quantize_pair("dec", 2)
-        unflip("dec", 2, "s")
-        stage1(4, 1)
-        respond(0, 0, 256, 0, "g")
-        quantize_z(0, 0, 256)
-        stage1(4, 0)
+        unflip("enc", 6, "s")
+        unmix(1, 1)
+        log_den()
+        inv_den()
+        stage1(1, 0)
+        quantize_pair("enc", 3)
+        widen(2, 0, "s")
+        stage1(1, 1)
+        quantize_v(1)
+        unit(1)
+        flip("dec", 1)
+        stage1(2, 0)
+        stage1(2, 1)
+        load_rows("dec", 1)
+        stage1(3, 0)
+        gain(0, "g")
+        gain(1, "g")
+        stage1(3, 1)
         unflip("dec", 0, "s")
-        unit(4)
-        respond(3, 0, 128, 1, "g")
-        stage2(0, 0, 256, 2)
-        stage2(1, 0, 256, 2)
-        stage2(0, 0, 256, 3)
-        stage1(5, 1)
-        respond(3, 0, 128, 0, "g")
-        quantize_pair("dec", 1)
-        finish(0, 0, 256, 3, "s")
+        mix(2, 0)
+        unit(2)
+        flip("dec", 2)
+        unit(3)
+        load_rows("dec", 2)
+        respond(0, 0, 256, 0, "v")
+        respond(0, 0, 256, 1, "v")
+        unflip("dec", 1, "s")
+        unmix(2, 0)
+        load_rows("dec", 3)
+        respond(1, 0, 256, 0, "v")
+        widen(2, 1, "s")
+        mix(2, 1)
+        widen(3, 0, "s")
+        unmix(2, 1)
+        flip("dec", 3)
+        unflip("dec", 2, "s")
+        flip("dec", 4)
+        flip("dec", 5)
+        quantize_z(0, 0, 256)
+        mix(3, 0)
         quantize_pair("dec", 0)
-        finish(0, 0, 256, 2, "s")
+        stage2(0, 0, 256, 0)
+        quantize_v(2)
+        stage1(4, 0)
+        unflip("dec", 3, "s")
+        stage1(4, 1)
+        unflip("dec", 4, "s")
+        unflip("dec", 5, "s")
+        quantize_pair("dec", 1)
+        unmix(3, 0)
+        flip("dec", 6)
+        unflip("dec", 6, "s")
         stage1(5, 0)
         stage2(0, 0, 256, 1)
-        stage2(0, 0, 256, 0)
-        finish(1, 0, 256, 2, "s")
+        flip("dec", 7)
+        widen(3, 1, "s")
+        respond(1, 0, 256, 1, "v")
+        quantize_pair("dec", 2)
+        unit(4)
+        stage1(5, 1)
+        unflip("dec", 7, "s")
+        unit(5)
+        respond(2, 0, 256, 0, "v")
+        quantize_pair("dec", 3)
+        finish(0, 0, 256, 0, "s")
+        respond(2, 0, 256, 1, "v")
+        mix(3, 1)
+        stage2(0, 0, 256, 2)
+        stage2(0, 0, 256, 3)
+        finish(0, 0, 256, 1, "s")
+        finish(0, 0, 256, 2, "s")
+        unmix(3, 1)
+        quantize_v(3)
+        quantize_z(1, 0, 256)
+        quantize_z(2, 0, 256)
+        finish(0, 0, 256, 3, "s")
+        store(0, 0, 256, 0)
+        stage1(6, 0)
+        stage1(6, 1)
+        stage2(1, 0, 256, 0)
+        stage2(1, 0, 256, 1)
+        unit(6)
+        finish(1, 0, 256, 0, "s")
+        finish(1, 0, 256, 1, "s")
+        stage2(1, 0, 256, 2)
         store(0, 0, 256, 1)
         stage2(1, 0, 256, 3)
-        finish(0, 0, 256, 0, "s")
-        stage2(1, 0, 256, 1)
-        finish(1, 0, 256, 3, "s")
-        finish(1, 0, 256, 1, "s")
-        finish(0, 0, 256, 1, "s")
-        respond(3, 128, 128, 0, "g")
-        unit(5)
-        quantize_z(3, 0, 128)
-        stage2(1, 0, 256, 0)
-        finish(1, 0, 256, 0, "s")
-        stage2(3, 0, 128, 0)
-        finish(3, 0, 128, 0, "s")
-        store(1, 0, 256, 1)
-        respond(3, 128, 128, 1, "g")
-        stage2(3, 0, 128, 1)
-        store(0, 0, 256, 0)
-        store(3, 0, 128, 0)
-        quantize_z(3, 128, 128)
-        respond(2, 0, 256, 0, "v")
+        stage2(2, 0, 256, 0)
+        stage1(7, 0)
+        respond(3, 0, 128, 0, "v")
         store(1, 0, 256, 0)
+        stage1(7, 1)
+        respond(3, 0, 128, 1, "v")
+        finish(1, 0, 256, 2, "s")
+        finish(1, 0, 256, 3, "s")
+        quantize_z(3, 0, 128)
+        store(1, 0, 256, 1)
+        unit(7)
+        stage2(2, 0, 256, 1)
+        respond(3, 128, 128, 0, "v")
+        respond(3, 128, 128, 1, "v")
+        stage2(2, 0, 256, 2)
+        finish(2, 0, 256, 0, "s")
+        finish(2, 0, 256, 1, "s")
+        stage2(2, 0, 256, 3)
+        stage2(3, 0, 128, 0)
+        stage2(3, 0, 128, 1)
+        quantize_z(3, 128, 128)
+        finish(2, 0, 256, 2, "s")
+        finish(2, 0, 256, 3, "s")
+        finish(3, 0, 128, 0, "s")
         stage2(3, 128, 128, 0)
         finish(3, 0, 128, 1, "s")
         finish(3, 128, 128, 0, "s")
-        respond(2, 0, 256, 1, "v")
         stage2(3, 128, 128, 1)
-        store(3, 0, 128, 1)
-        quantize_z(2, 0, 256)
-        stage2(2, 0, 256, 3)
         finish(3, 128, 128, 1, "s")
-        finish(2, 0, 256, 3, "s")
-        store(3, 128, 128, 1)
-        stage2(2, 0, 256, 2)
-        stage2(2, 0, 256, 0)
-        store(3, 128, 128, 0)
-        finish(2, 0, 256, 2, "s")
-        store(2, 0, 256, 1)
-        finish(2, 0, 256, 0, "s")
-        stage2(2, 0, 256, 1)
-        finish(2, 0, 256, 1, "s")
         store(2, 0, 256, 0)
+        store(2, 0, 256, 1)
+        store(3, 0, 128, 0)
+        store(3, 0, 128, 1)
+        store(3, 128, 128, 0)
+        store(3, 128, 128, 1)

@@ -52,10 +52,10 @@ def tile_laplacepoleresidueoperator_kernel(tc, v_bytes, v_scale, enc, dec, alpha
         E = keep.tile([P, PACK, D], F32, name="E")
         sp = keep.tile([P, PACK, D], F32, name="sp")
         W = keep.tile([P, PACK, D], F32, name="W")
-        G = keep.tile([P, D, PACK], F32, name="G")
+        G = keep.tile([P, PACK, D], F32, name="G")
         Gb = []
         for g in range(2):
-            Gb.append(keep.tile([P, D, PACK], F32, name="Gb%d" % g))
+            Gb.append(keep.tile([P, PACK, D], F32, name="Gb%d" % g))
         capped = keep.tile([P, PACK, D], BF16, name="capped")
         omf = keep.tile([P, PACK], F32, name="omf")
         nom = keep.tile([P, PACK], F32, name="nom")
@@ -197,11 +197,11 @@ def tile_laplacepoleresidueoperator_kernel(tc, v_bytes, v_scale, enc, dec, alpha
                 nc.scalar.activation(out=W[:, t], in_=W[:, t], func=ACT.Ln, bias=om2[:, t : t + 1])
 
         def inv_den():
-            nc.scalar.activation(out=G[:], in_=W[:].rearrange("p t d -> p d t"), func=ACT.Exp, scale=-1.0)
+            nc.scalar.activation(out=G[:], in_=W[:], func=ACT.Exp, scale=-1.0)
 
         def gain(g, engine):
             eng = nc.gpsimd if engine == "g" else nc.vector
-            eng.tensor_tensor(out=Gb[g][:], in0=G[:], in1=be[:, g].rearrange("p t d -> p d t"), op=ALU.mult)
+            eng.tensor_tensor(out=Gb[g][:], in0=G[:], in1=be[:, g], op=ALU.mult)
 
         def rotate_a(k, h):
             b, ts, ds = shape(k)
@@ -233,9 +233,9 @@ def tile_laplacepoleresidueoperator_kernel(tc, v_bytes, v_scale, enc, dec, alpha
                 z[b, n0] = work.tile([P, 2, nd * PACK], BF16, name="z%d" % nd, align_bytes=64)
             eng = nc.gpsimd if engine == "g" else nc.vector
             eng.tensor_tensor(
-                out=z[b, n0][:, g].rearrange("p (n t) -> p n t", t=PACK),
-                in0=us[b][:, g, :, n0 : n0 + nd].rearrange("p t n -> p n t"),
-                in1=Gb[g][:, n0 : n0 + nd, :],
+                out=z[b, n0][:, g].rearrange("p (c i t) -> p c t i", i=4, t=PACK),
+                in0=us[b][:, g, :, n0 : n0 + nd].rearrange("p t (c i) -> p c t i", i=4),
+                in1=Gb[g][:, :, n0 : n0 + nd].rearrange("p t (c i) -> p c t i", i=4),
                 op=ALU.mult,
             )
 

@@ -39,7 +39,6 @@ def tile_laplacepoleresidueoperator_kernel(tc, v_bytes, v_scale, enc, dec, alpha
         om = keep.tile([P, PACK], BF16, name="om")
         warm = keep.tile([P, 2], F32, name="warm")
         ident = keep.tile([P, P], F32, name="ident")
-        ident_b = keep.tile([P, P], BF16, name="ident_b")
         al = keep.tile([P, PACK, D], BF16, name="al")
         be = keep.tile([P, 2, PACK, D], BF16, name="be")
         v_raw = []
@@ -73,7 +72,6 @@ def tile_laplacepoleresidueoperator_kernel(tc, v_bytes, v_scale, enc, dec, alpha
             nc.vector.memset(warm[:], 0.0)
             nc.scalar.activation(out=warm[:, 1:2], in_=warm[:, 0:1], func=ACT.Exp)
             make_identity(nc, ident[:])
-            make_identity(nc, ident_b[:])
             nc.gpsimd.tensor_scalar(out=omf[:], in0=om[:], scalar1=1.0, scalar2=0.0, op0=ALU.mult, op1=ALU.add)
             nc.gpsimd.tensor_scalar(out=nom[:], in0=om[:], scalar1=-1.0, scalar2=0.0, op0=ALU.mult, op1=ALU.add)
             nc.gpsimd.tensor_tensor(out=om2[:], in0=om[:], in1=om[:], op=ALU.mult)
@@ -121,7 +119,7 @@ def tile_laplacepoleresidueoperator_kernel(tc, v_bytes, v_scale, enc, dec, alpha
 
         def widen(b, g, engine):
             if b not in wide:
-                wide[b] = work.tile([P, 2, PACK, D], BF16, name="wide")
+                wide[b] = work.tile([P, 2, PACK, D], BF16, name="wide", bufs=3)
             for t in range(PACK):
                 src = v_raw[b][:, g, t, :].bitcast(FP8)
                 if engine == "v":
@@ -129,22 +127,16 @@ def tile_laplacepoleresidueoperator_kernel(tc, v_bytes, v_scale, enc, dec, alpha
                 else:
                     nc.scalar.activation(out=wide[b][:, g, t, :], in_=src, func=ACT.Copy, scale=v_sc[:, g, t : t + 1])
 
-        def mix(b, g):
-            bank = psum.tile([P, PACK, D], BF16, name="bank")
-            for q in range(2):
-                nc.tensor.matmul(
-                    bank[:, 2 * q : 2 * q + 2, :].rearrange("p t d -> p (t d)"),
-                    lhsT=ident_b[:],
-                    rhs=wide[b][:, g, 2 * q : 2 * q + 2, :].rearrange("p t d -> p (t d)"),
-                    start=True,
-                    stop=True,
-                )
-            banks["mix", b, g] = bank
-
-        def unmix(b, g):
+        def mix(b, g, engine):
             if b not in mixed:
-                mixed[b] = work.tile([P, 2, D, PACK], BF16, name="mixed", align_bytes=64)
-            nc.scalar.copy(out=mixed[b][:, g], in_=banks["mix", b, g][:].rearrange("p t d -> p d t"))
+                mixed[b] = work.tile([P, 2, D, PACK], BF16, name="mixed", bufs=3, align_bytes=64)
+            dst, src = mixed[b][:, g], wide[b][:, g].rearrange("p t d -> p d t")
+            if engine == "v":
+                nc.vector.tensor_copy(out=dst, in_=src)
+            elif engine == "g":
+                nc.gpsimd.tensor_scalar(out=dst, in0=src, scalar1=1.0, scalar2=0.0, op0=ALU.mult, op1=ALU.add)
+            else:
+                nc.scalar.copy(out=dst, in_=src)
 
         def quantize_v(b):
             quantize(("v", b), mixed[b][:].rearrange("p g d t -> p (g d t)"))
@@ -206,7 +198,7 @@ def tile_laplacepoleresidueoperator_kernel(tc, v_bytes, v_scale, enc, dec, alpha
         def rotate_a(k, h):
             b, ts, ds = shape(k)
             if b not in us:
-                us[b] = work.tile([P, 2, PACK, D], F32, name="u")
+                us[b] = work.tile([P, 2, PACK, D], F32, name="u", bufs=3)
             nc.vector.tensor_tensor(out=us[b][:, h, ts, ds], in0=banks["c", k, h][:], in1=sp[:, ts, ds], op=ALU.mult)
 
         def rotate_b(k, h):
@@ -271,171 +263,163 @@ def tile_laplacepoleresidueoperator_kernel(tc, v_bytes, v_scale, enc, dec, alpha
         cap()
         expo()
         load_v(0)
-        load_rows("enc", 0)
         widen(0, 0, "v")
-        flip("enc", 0)
-        flip("enc", 1)
-        loga()
-        mix(0, 0)
         widen(0, 1, "v")
-        mix(0, 1)
+        load_rows("enc", 0)
+        flip("enc", 0)
         load_rows("enc", 2)
-        unmix(0, 0)
+        mix(0, 0, "v")
+        flip("enc", 1)
         flip("enc", 4)
-        unmix(0, 1)
-        load_rows("enc", 1)
         flip("enc", 5)
         unflip("enc", 0, "v")
+        load_rows("enc", 1)
+        flip("enc", 2)
         unflip("enc", 1, "v")
-        unflip("enc", 4, "s")
+        flip("enc", 3)
         load_rows("enc", 3)
         load_v(1)
-        quantize_pair("enc", 0)
-        flip("enc", 2)
-        flip("enc", 3)
-        flip("enc", 6)
-        unflip("enc", 5, "s")
-        softplus()
-        quantize_v(0)
         load_beta()
+        loga()
+        unflip("enc", 4, "s")
+        unflip("enc", 5, "s")
         unflip("enc", 3, "s")
-        widen(1, 0, "v")
-        square()
-        quantize_pair("enc", 2)
-        load_v(2)
-        load_v(3)
+        widen(1, 0, "s")
+        flip("enc", 6)
         flip("enc", 7)
-        widen(1, 1, "v")
-        stage1(0, 0)
-        stage1(0, 1)
-        unit(0)
-        unflip("enc", 7, "s")
+        load_v(2)
+        mix(0, 1, "g")
+        quantize_v(0)
+        softplus()
+        square()
+        quantize_pair("enc", 0)
+        quantize_pair("enc", 2)
+        load_v(3)
         load_rows("dec", 0)
-        unflip("enc", 2, "s")
-        mix(1, 0)
-        unmix(1, 0)
-        quantize_pair("enc", 1)
-        mix(1, 1)
-        flip("dec", 0)
-        unflip("enc", 6, "s")
-        unmix(1, 1)
+        widen(1, 1, "v")
+        load_rows("dec", 1)
+        unflip("enc", 7, "s")
+        unflip("enc", 2, "v")
+        unflip("enc", 6, "v")
         log_den()
         inv_den()
+        stage1(0, 0)
+        widen(2, 0, "s")
+        stage1(0, 1)
+        quantize_pair("enc", 1)
         stage1(1, 0)
         quantize_pair("enc", 3)
-        widen(2, 0, "s")
-        stage1(1, 1)
-        quantize_v(1)
-        unit(1)
-        flip("dec", 1)
-        stage1(2, 0)
-        stage1(2, 1)
-        load_rows("dec", 1)
-        stage1(3, 0)
+        mix(1, 0, "g")
+        mix(1, 1, "g")
         gain(0, "g")
-        gain(1, "g")
-        stage1(3, 1)
-        unflip("dec", 0, "s")
-        mix(2, 0)
-        unit(2)
-        flip("dec", 2)
-        unit(3)
-        load_rows("dec", 2)
-        respond(0, 0, 256, 0, "v")
-        respond(0, 0, 256, 1, "v")
-        unflip("dec", 1, "s")
-        unmix(2, 0)
-        load_rows("dec", 3)
-        respond(1, 0, 256, 0, "v")
+        stage1(1, 1)
         widen(2, 1, "s")
-        mix(2, 1)
-        widen(3, 0, "s")
-        unmix(2, 1)
-        flip("dec", 3)
-        unflip("dec", 2, "s")
-        flip("dec", 4)
-        flip("dec", 5)
-        quantize_z(0, 0, 256)
-        mix(3, 0)
-        quantize_pair("dec", 0)
-        stage2(0, 0, 256, 0)
+        quantize_v(1)
+        stage1(2, 0)
+        flip("dec", 0)
+        unflip("dec", 0, "s")
+        flip("dec", 1)
+        stage1(2, 1)
+        gain(1, "g")
+        unit(0)
+        load_rows("dec", 2)
+        unit(1)
+        stage1(3, 0)
+        load_rows("dec", 3)
+        mix(2, 0, "s")
+        mix(2, 1, "s")
+        flip("dec", 2)
+        unit(2)
+        stage1(3, 1)
+        unflip("dec", 1, "s")
+        unit(3)
         quantize_v(2)
-        stage1(4, 0)
+        unflip("dec", 2, "s")
+        flip("dec", 3)
+        respond(0, 0, 256, 0, "g")
         unflip("dec", 3, "s")
+        flip("dec", 4)
+        widen(3, 0, "s")
+        stage1(4, 0)
+        quantize_pair("dec", 0)
+        mix(3, 0, "s")
         stage1(4, 1)
-        unflip("dec", 4, "s")
-        unflip("dec", 5, "s")
-        quantize_pair("dec", 1)
-        unmix(3, 0)
-        flip("dec", 6)
-        unflip("dec", 6, "s")
+        flip("dec", 5)
         stage1(5, 0)
-        stage2(0, 0, 256, 1)
-        flip("dec", 7)
-        widen(3, 1, "s")
-        respond(1, 0, 256, 1, "v")
-        quantize_pair("dec", 2)
-        unit(4)
+        unflip("dec", 4, "s")
         stage1(5, 1)
-        unflip("dec", 7, "s")
+        respond(0, 0, 256, 1, "g")
+        widen(3, 1, "s")
+        flip("dec", 6)
+        quantize_pair("dec", 1)
+        quantize_z(0, 0, 256)
+        mix(3, 1, "s")
+        unit(4)
+        unflip("dec", 5, "s")
+        flip("dec", 7)
         unit(5)
-        respond(2, 0, 256, 0, "v")
-        quantize_pair("dec", 3)
+        unflip("dec", 6, "s")
+        unflip("dec", 7, "s")
+        respond(1, 0, 256, 0, "g")
+        respond(1, 0, 256, 1, "g")
+        stage2(0, 0, 256, 0)
+        stage2(0, 0, 256, 1)
+        quantize_pair("dec", 2)
         finish(0, 0, 256, 0, "s")
-        respond(2, 0, 256, 1, "v")
-        mix(3, 1)
         stage2(0, 0, 256, 2)
-        stage2(0, 0, 256, 3)
         finish(0, 0, 256, 1, "s")
-        finish(0, 0, 256, 2, "s")
-        unmix(3, 1)
-        quantize_v(3)
-        quantize_z(1, 0, 256)
-        quantize_z(2, 0, 256)
-        finish(0, 0, 256, 3, "s")
         store(0, 0, 256, 0)
+        quantize_v(3)
+        quantize_pair("dec", 3)
+        quantize_z(1, 0, 256)
+        finish(0, 0, 256, 2, "s")
         stage1(6, 0)
+        stage2(0, 0, 256, 3)
+        respond(2, 0, 256, 0, "v")
+        respond(2, 0, 256, 1, "g")
         stage1(6, 1)
         stage2(1, 0, 256, 0)
         stage2(1, 0, 256, 1)
         unit(6)
-        finish(1, 0, 256, 0, "s")
-        finish(1, 0, 256, 1, "s")
+        finish(0, 0, 256, 3, "s")
         stage2(1, 0, 256, 2)
-        store(0, 0, 256, 1)
-        stage2(1, 0, 256, 3)
-        stage2(2, 0, 256, 0)
+        respond(3, 0, 128, 0, "g")
         stage1(7, 0)
-        respond(3, 0, 128, 0, "v")
-        store(1, 0, 256, 0)
+        finish(1, 0, 256, 0, "s")
+        quantize_z(2, 0, 256)
+        finish(1, 0, 256, 1, "s")
+        respond(3, 0, 128, 1, "g")
+        stage2(1, 0, 256, 3)
         stage1(7, 1)
-        respond(3, 0, 128, 1, "v")
-        finish(1, 0, 256, 2, "s")
-        finish(1, 0, 256, 3, "s")
-        quantize_z(3, 0, 128)
-        store(1, 0, 256, 1)
         unit(7)
+        finish(1, 0, 256, 2, "s")
+        store(0, 0, 256, 1)
+        finish(1, 0, 256, 3, "s")
+        stage2(2, 0, 256, 0)
         stage2(2, 0, 256, 1)
-        respond(3, 128, 128, 0, "v")
-        respond(3, 128, 128, 1, "v")
-        stage2(2, 0, 256, 2)
         finish(2, 0, 256, 0, "s")
         finish(2, 0, 256, 1, "s")
+        store(1, 0, 256, 0)
+        quantize_z(3, 0, 128)
+        stage2(2, 0, 256, 2)
         stage2(2, 0, 256, 3)
+        respond(3, 128, 128, 0, "v")
+        respond(3, 128, 128, 1, "v")
         stage2(3, 0, 128, 0)
-        stage2(3, 0, 128, 1)
+        store(1, 0, 256, 1)
         quantize_z(3, 128, 128)
         finish(2, 0, 256, 2, "s")
         finish(2, 0, 256, 3, "s")
         finish(3, 0, 128, 0, "s")
-        stage2(3, 128, 128, 0)
-        finish(3, 0, 128, 1, "s")
-        finish(3, 128, 128, 0, "s")
-        stage2(3, 128, 128, 1)
-        finish(3, 128, 128, 1, "s")
         store(2, 0, 256, 0)
+        stage2(3, 0, 128, 1)
+        finish(3, 0, 128, 1, "s")
+        stage2(3, 128, 128, 0)
+        finish(3, 128, 128, 0, "s")
         store(2, 0, 256, 1)
         store(3, 0, 128, 0)
         store(3, 0, 128, 1)
         store(3, 128, 128, 0)
+        stage2(3, 128, 128, 1)
+        finish(3, 128, 128, 1, "s")
         store(3, 128, 128, 1)

from contextlib import ExitStack

import concourse.mybir as mybir
from concourse.masks import make_identity

B, N, D, M = 4, 1024, 256, 512
M2 = 2 * M
P = 128
PACK = 4
HALF = 128

FLOPS = 2 * B * D * (M2 * N + N * M2)

F32 = mybir.dt.float32
BF16 = mybir.dt.bfloat16
U32 = mybir.dt.uint32
U8 = mybir.dt.uint8
FP8 = mybir.dt.float8_e4m3fn
FP8X4 = mybir.dt.float8_e4m3fn_x4
ACT = mybir.ActivationFunctionType
ALU = mybir.AluOpType

ALPHA_CAP = 40.0


def tile_laplacepoleresidueoperator_kernel(tc, v_bytes, v_scale, enc, dec, alpha, omega, beta, out):
    nc = tc.nc
    enc_rows = enc.rearrange("(h p t) k -> h p t k", h=2, t=PACK)
    dec_rows = dec.rearrange("(p j) k -> p j k", j=8)
    out_rows = out.rearrange("b (p j) d -> b p j d", j=8)

    with ExitStack() as ctx:
        keep = ctx.enter_context(tc.tile_pool(name="keep", bufs=1))
        work = ctx.enter_context(tc.tile_pool(name="work", bufs=2))
        psum = ctx.enter_context(tc.psum_pool(name="psum", bufs=8))
        ctx.enter_context(tc.manual_schedule())

        v_sc = keep.tile([P, 2, PACK], F32, name="v_sc")
        om = keep.tile([P, PACK], BF16, name="om")
        warm = keep.tile([P, 2], F32, name="warm")
        ident = keep.tile([P, P], F32, name="ident")
        al = keep.tile([P, PACK, D], BF16, name="al")
        be = keep.tile([P, 2, PACK, D], BF16, name="be")
        v_raw = []
        for b in range(B):
            v_raw.append(keep.tile([P, 2, PACK, D], U8, name="v_raw%d" % b))
        raw = {}
        for i in range(4):
            raw["enc", i] = keep.tile([P, 2, N], BF16, name="enc_raw%d" % i)
            raw["dec", i] = keep.tile([P, 2, M2], BF16, name="dec_raw%d" % i)
        E = keep.tile([P, PACK, D], F32, name="E")
        sp = keep.tile([P, PACK, D], F32, name="sp")
        W = keep.tile([P, PACK, D], F32, name="W")
        G = keep.tile([P, PACK, D], F32, name="G")
        Gb = []
        for g in range(2):
            Gb.append(keep.tile([P, PACK, D], F32, name="Gb%d" % g))
        capped = keep.tile([P, PACK, D], BF16, name="capped")
        omf = keep.tile([P, PACK], F32, name="omf")
        nom = keep.tile([P, PACK], F32, name="nom")
        om2 = keep.tile([P, PACK], F32, name="om2")

        banks, pairs, codes, scales, wide, mixed, us, z, results = {}, {}, {}, {}, {}, {}, {}, {}, {}
        for kind in ("enc", "dec", "v", "z"):
            for i in range(4):
                codes[kind, i] = keep.tile([P, 2 * D], U32, name="c_%s_%d" % (kind, i), align_bytes=64)
                scales[kind, i] = keep.tile([P, 2 * D], U8, name="s_%s_%d" % (kind, i), align_bytes=64)

        def setup():
            nc.scalar.dma_start(out=v_sc[:], in_=v_scale.rearrange("o (g p t) x -> p (o g) (t x)", p=P, t=PACK))
            nc.scalar.dma_start(out=om[:], in_=omega.rearrange("(p t) -> p t", t=PACK))
            nc.vector.memset(warm[:], 0.0)
            nc.scalar.activation(out=warm[:, 1:2], in_=warm[:, 0:1], func=ACT.Exp)
            make_identity(nc, ident[:])
            nc.gpsimd.tensor_scalar(out=omf[:], in0=om[:], scalar1=1.0, scalar2=0.0, op0=ALU.mult, op1=ALU.add)
            nc.gpsimd.tensor_scalar(out=nom[:], in0=om[:], scalar1=-1.0, scalar2=0.0, op0=ALU.mult, op1=ALU.add)
            nc.gpsimd.tensor_tensor(out=om2[:], in0=om[:], in1=om[:], op=ALU.mult)

        def load_alpha():
            nc.sync.dma_start(out=al[:], in_=alpha.rearrange("(p t) d -> p t d", t=PACK))

        def load_beta():
            nc.sync.dma_start(out=be[:], in_=beta.rearrange("(g p t) d -> p g t d", p=P, t=PACK))

        def load_v(b):
            nc.sync.dma_start(
                out=v_raw[b][:].rearrange("p g t d -> p g (t d)"),
                in_=v_bytes[b].rearrange("(g p t) d -> p g (t d)", p=P, t=PACK),
            )

        def load_rows(kind, i):
            j = 2 * (i % 2) if kind == "enc" else 2 * i
            src = (enc_rows[i // 2] if kind == "enc" else dec_rows)[:, j : j + 2, :]
            nc.sync.dma_start(out=raw[kind, i][:], in_=src)

        def flip(kind, i):
            bank = psum.tile([P, 2, 2, P], F32, name="bank")
            words = raw[kind, i // 2][:, i % 2].bitcast(F32)
            for g in range(2):
                for u in range(2):
                    nc.tensor.transpose(bank[:, g, u, :], words[:, 256 * g + u : 256 * (g + 1) : 2], ident[:])
            banks[kind, i] = bank

        def unflip(kind, i, engine):
            if (kind, i // 2) not in pairs:
                pairs[kind, i // 2] = work.tile([P, 2, 2, P, PACK], BF16, name="pair", bufs=4, align_bytes=64)
            dst = pairs[kind, i // 2][:, i % 2].bitcast(F32)
            src = banks[kind, i][:].rearrange("p g u m -> p g m u")
            if engine == "v":
                nc.vector.tensor_copy(out=dst, in_=src)
            else:
                nc.scalar.copy(out=dst, in_=src)

        def quantize(key, src, cols=slice(0, 2 * D)):
            nc.vector.quantize_mx(out=codes[key][:, cols].bitcast(FP8X4), scales=scales[key][:, cols], in_=src)

        def quantize_pair(kind, i):
            quantize((kind, i), pairs[kind, i][:].rearrange("p e g m t -> p (e g m t)"))

        def widen(b, g, engine):
            if b not in wide:
                wide[b] = work.tile([P, 2, PACK, D], BF16, name="wide", bufs=3)
            for t in range(PACK):
                src = v_raw[b][:, g, t, :].bitcast(FP8)
                if engine == "v":
                    nc.vector.tensor_scalar(out=wide[b][:, g, t, :], in0=src, scalar1=v_sc[:, g, t : t + 1], scalar2=None, op0=ALU.mult)
                else:
                    nc.scalar.activation(out=wide[b][:, g, t, :], in_=src, func=ACT.Copy, scale=v_sc[:, g, t : t + 1])

        def mix(b, g, engine):
            if b not in mixed:
                mixed[b] = work.tile([P, 2, D, PACK], BF16, name="mixed", bufs=3, align_bytes=64)
            dst, src = mixed[b][:, g], wide[b][:, g].rearrange("p t d -> p d t")
            if engine == "v":
                nc.vector.tensor_copy(out=dst, in_=src)
            elif engine == "g":
                nc.gpsimd.tensor_scalar(out=dst, in0=src, scalar1=1.0, scalar2=0.0, op0=ALU.mult, op1=ALU.add)
            else:
                nc.scalar.copy(out=dst, in_=src)

        def quantize_v(b):
            quantize(("v", b), mixed[b][:].rearrange("p g d t -> p (g d t)"))

        def shape(k):
            b = k // 2
            if b < 3:
                return b, slice(2 * (k % 2), 2 * (k % 2) + 2), slice(0, D)
            return b, slice(0, PACK), slice((k % 2) * HALF, (k % 2 + 1) * HALF)

        def product(bank, i, kind, row, src, cols0, width):
            for g in range(2):
                w = slice((row % 2) * 256 + g * P, (row % 2) * 256 + (g + 1) * P)
                c = slice(g * D + cols0, g * D + cols0 + width)
                nc.tensor.matmul_mx(
                    out=bank[:, i, :],
                    lhsT=codes[kind, row // 2][:, w].bitcast(FP8X4),
                    lhsT_scale=scales[kind, row // 2][:, w],
                    rhs=codes[src][:, c].bitcast(FP8X4),
                    rhs_scale=scales[src][:, c],
                    start=(g == 0),
                    stop=(g == 1),
                )

        def stage1(k, h):
            b, ts, ds = shape(k)
            nt, nd = ts.stop - ts.start, ds.stop - ds.start
            bank = psum.tile([P, nt, nd], F32, name="bank")
            for i in range(nt):
                product(bank, i, "enc", 4 * h + ts.start + i, ("v", b), ds.start, nd)
            banks["c", k, h] = bank

        def cap():
            nc.vector.tensor_scalar(out=capped[:], in0=al[:], scalar1=ALPHA_CAP, scalar2=None, op0=ALU.min)

        def expo():
            nc.scalar.activation(out=E[:], in_=capped[:], func=ACT.Exp)

        def loga():
            nc.scalar.activation(out=E[:], in_=E[:], func=ACT.Ln, bias=1.0)

        def softplus():
            nc.vector.tensor_tensor(out=sp[:], in0=E[:], in1=al[:], op=ALU.max)

        def square():
            nc.scalar.activation(out=W[:], in_=sp[:], func=ACT.Square)

        def log_den():
            for t in range(PACK):
                nc.scalar.activation(out=W[:, t], in_=W[:, t], func=ACT.Ln, bias=om2[:, t : t + 1])

        def inv_den():
            nc.scalar.activation(out=G[:], in_=W[:], func=ACT.Exp, scale=-1.0)

        def gain(g, engine):
            eng = nc.gpsimd if engine == "g" else nc.vector
            eng.tensor_tensor(out=Gb[g][:], in0=G[:], in1=be[:, g], op=ALU.mult)

        def rotate_a(k, h):
            b, ts, ds = shape(k)
            if b not in us:
                us[b] = work.tile([P, 2, PACK, D], F32, name="u", bufs=3)
            nc.vector.tensor_tensor(out=us[b][:, h, ts, ds], in0=banks["c", k, h][:], in1=sp[:, ts, ds], op=ALU.mult)

        def rotate_b(k, h):
            b, ts, ds = shape(k)
            other = banks["c", k, 1 - h]
            for t in range(ts.start, ts.stop):
                nc.vector.scalar_tensor_tensor(
                    out=us[b][:, h, t, ds],
                    in0=other[:, t - ts.start, :],
                    scalar=(omf, nom)[h][:, t : t + 1],
                    in1=us[b][:, h, t, ds],
                    op0=ALU.mult,
                    op1=ALU.add,
                )

        def unit(k):
            for h in range(2):
                rotate_a(k, h)
            for h in range(2):
                rotate_b(k, h)

        def respond(b, n0, nd, g, engine):
            if (b, n0) not in z:
                z[b, n0] = work.tile([P, 2, nd * PACK], BF16, name="z%d" % nd, align_bytes=64)
            eng = nc.gpsimd if engine == "g" else nc.vector
            eng.tensor_tensor(
                out=z[b, n0][:, g].rearrange("p (c i t) -> p c t i", i=4, t=PACK),
                in0=us[b][:, g, :, n0 : n0 + nd].rearrange("p t (c i) -> p c t i", i=4),
                in1=Gb[g][:, :, n0 : n0 + nd].rearrange("p t (c i) -> p c t i", i=4),
                op=ALU.mult,
            )

        def quantize_z(b, n0, nd):
            if nd == D:
                quantize(("z", b), z[b, n0][:].rearrange("p g n -> p (g n)"))
            else:
                for g in range(2):
                    quantize(("z", b), z[b, n0][:, g, :], slice(g * D + n0, g * D + n0 + nd))

        def stage2(b, n0, width, q):
            per = 512 // width
            bank = psum.tile([P, per, width], F32, name="bank")
            for i in range(per):
                product(bank, i, "dec", q * per + i, ("z", b), n0, width)
            banks["o", b, n0, q] = bank

        def finish(b, n0, width, q, engine):
            if (b, n0) not in results:
                results[b, n0] = work.tile([P, 8, width], F32, name="res%d" % width, bufs=2)
            per = 512 // width
            dst, src = results[b, n0][:, q * per : (q + 1) * per, :], banks["o", b, n0, q][:]
            if engine == "v":
                nc.vector.tensor_copy(out=dst, in_=src)
            else:
                nc.scalar.copy(out=dst, in_=src)

        def store(b, n0, width, s):
            nc.sync.dma_start(out=out_rows[b][:, 4 * s : 4 * s + 4, n0 : n0 + width], in_=results[b, n0][:, 4 * s : 4 * s + 4, :])

        setup()
        load_alpha()
        cap()
        expo()
        load_v(0)
        widen(0, 0, "v")
        widen(0, 1, "v")
        load_rows("enc", 0)
        flip("enc", 0)
        load_rows("enc", 2)
        mix(0, 0, "v")
        flip("enc", 1)
        flip("enc", 4)
        flip("enc", 5)
        unflip("enc", 0, "v")
        load_rows("enc", 1)
        flip("enc", 2)
        unflip("enc", 1, "v")
        flip("enc", 3)
        load_rows("enc", 3)
        load_v(1)
        load_beta()
        loga()
        unflip("enc", 4, "s")
        unflip("enc", 5, "s")
        unflip("enc", 3, "s")
        widen(1, 0, "s")
        flip("enc", 6)
        flip("enc", 7)
        load_v(2)
        mix(0, 1, "g")
        quantize_v(0)
        softplus()
        square()
        quantize_pair("enc", 0)
        quantize_pair("enc", 2)
        load_v(3)
        load_rows("dec", 0)
        widen(1, 1, "v")
        load_rows("dec", 1)
        unflip("enc", 7, "s")
        unflip("enc", 2, "v")
        unflip("enc", 6, "v")
        log_den()
        inv_den()
        stage1(0, 0)
        widen(2, 0, "s")
        stage1(0, 1)
        quantize_pair("enc", 1)
        stage1(1, 0)
        quantize_pair("enc", 3)
        mix(1, 0, "g")
        mix(1, 1, "g")
        gain(0, "g")
        stage1(1, 1)
        widen(2, 1, "s")
        quantize_v(1)
        stage1(2, 0)
        flip("dec", 0)
        unflip("dec", 0, "s")
        flip("dec", 1)
        stage1(2, 1)
        gain(1, "g")
        unit(0)
        load_rows("dec", 2)
        unit(1)
        stage1(3, 0)
        load_rows("dec", 3)
        mix(2, 0, "s")
        mix(2, 1, "s")
        flip("dec", 2)
        unit(2)
        stage1(3, 1)
        unflip("dec", 1, "s")
        unit(3)
        quantize_v(2)
        unflip("dec", 2, "s")
        flip("dec", 3)
        respond(0, 0, 256, 0, "g")
        unflip("dec", 3, "s")
        flip("dec", 4)
        widen(3, 0, "s")
        stage1(4, 0)
        quantize_pair("dec", 0)
        mix(3, 0, "s")
        stage1(4, 1)
        flip("dec", 5)
        stage1(5, 0)
        unflip("dec", 4, "s")
        stage1(5, 1)
        respond(0, 0, 256, 1, "g")
        widen(3, 1, "s")
        flip("dec", 6)
        quantize_pair("dec", 1)
        quantize_z(0, 0, 256)
        mix(3, 1, "s")
        unit(4)
        unflip("dec", 5, "s")
        flip("dec", 7)
        unit(5)
        unflip("dec", 6, "s")
        unflip("dec", 7, "s")
        respond(1, 0, 256, 0, "g")
        respond(1, 0, 256, 1, "g")
        stage2(0, 0, 256, 0)
        stage2(0, 0, 256, 1)
        quantize_pair("dec", 2)
        finish(0, 0, 256, 0, "s")
        stage2(0, 0, 256, 2)
        finish(0, 0, 256, 1, "s")
        store(0, 0, 256, 0)
        quantize_v(3)
        quantize_pair("dec", 3)
        quantize_z(1, 0, 256)
        finish(0, 0, 256, 2, "s")
        stage1(6, 0)
        stage2(0, 0, 256, 3)
        respond(2, 0, 256, 0, "v")
        respond(2, 0, 256, 1, "g")
        stage1(6, 1)
        stage2(1, 0, 256, 0)
        stage2(1, 0, 256, 1)
        unit(6)
        finish(0, 0, 256, 3, "s")
        stage2(1, 0, 256, 2)
        respond(3, 0, 128, 0, "g")
        stage1(7, 0)
        finish(1, 0, 256, 0, "s")
        quantize_z(2, 0, 256)
        finish(1, 0, 256, 1, "s")
        respond(3, 0, 128, 1, "g")
        stage2(1, 0, 256, 3)
        stage1(7, 1)
        unit(7)
        finish(1, 0, 256, 2, "s")
        store(0, 0, 256, 1)
        finish(1, 0, 256, 3, "s")
        stage2(2, 0, 256, 0)
        stage2(2, 0, 256, 1)
        finish(2, 0, 256, 0, "s")
        finish(2, 0, 256, 1, "s")
        store(1, 0, 256, 0)
        quantize_z(3, 0, 128)
        stage2(2, 0, 256, 2)
        stage2(2, 0, 256, 3)
        respond(3, 128, 128, 0, "v")
        respond(3, 128, 128, 1, "v")
        stage2(3, 0, 128, 0)
        store(1, 0, 256, 1)
        quantize_z(3, 128, 128)
        finish(2, 0, 256, 2, "s")
        finish(2, 0, 256, 3, "s")
        finish(3, 0, 128, 0, "s")
        store(2, 0, 256, 0)
        stage2(3, 0, 128, 1)
        finish(3, 0, 128, 1, "s")
        stage2(3, 128, 128, 0)
        finish(3, 128, 128, 0, "s")
        store(2, 0, 256, 1)
        store(3, 0, 128, 0)
        store(3, 0, 128, 1)
        store(3, 128, 128, 0)
        stage2(3, 128, 128, 1)
        finish(3, 128, 128, 1, "s")
        store(3, 128, 128, 1)
